import numpy as np
import ml_dtypes


def mxq(x, axis, fmt="e4m3"):
    dtype, down = {"e4m3": (ml_dtypes.float8_e4m3fn, 7), "e5m2": (ml_dtypes.float8_e5m2, 14)}[fmt]
    v = np.moveaxis(np.asarray(x, np.float32).astype(ml_dtypes.bfloat16).astype(np.float64), axis, -1)
    blocks = v.reshape(v.shape[:-1] + (-1, 32))
    amax = np.abs(blocks).max(-1, keepdims=True)
    byte = np.maximum(np.where(amax > 0, np.frexp(amax)[1] - 1 + 127, 0) - down, 1)
    scale = np.exp2(byte - 127.0)
    codes = (blocks / scale).astype(np.float32).astype(dtype).astype(np.float64)
    return np.moveaxis((codes * scale).reshape(v.shape), -1, axis)


WIDE = False


def mx_kscale(k):
    if not WIDE:
        return np.ones(k)
    levels = np.array([10, -10, 5, -5, 0])
    if k % 512:
        return np.exp2(np.random.permutation(np.resize(levels, k // 32))).repeat(32)
    a = np.empty((k // 512, 16))
    for p in range(k // 512):
        a[p, :8] = np.random.permutation(np.resize(levels, 8))
        for g in range(8):
            far = levels[np.abs(levels - a[p, g]) >= 10]
            a[p, g + 8] = far[np.random.randint(len(far))]
    return np.exp2(a.ravel()).repeat(32)


def f64(x):
    return np.asarray(x).astype(np.float64)


def striped(idx):
    return np.tile(idx.reshape(-1, 16).T, (8, 1)).astype(np.uint16)


def unstriped(offs):
    return offs[:16].T.reshape(-1).astype(np.int64)


def relu(v):
    return np.maximum(v, 0.0)


K, T, D, S, V, R, N = 512, 4096, 3, 3072, 1024, 4, 512


def setup_inputs():
    n = np.random.standard_normal
    s = mx_kscale(K)[:, None]
    return {
        "xT": (n((K, T)) * s).astype(np.float32),
        "w": (n((D, K, N)) / np.sqrt(D * K) / s[None]).astype(np.float32),
        "b": (0.3 * n((N, 1))).astype(np.float32),
        "offs": striped(np.concatenate([R * np.arange(V) + np.random.randint(0, R, V) for _ in range(D)])),
    }


def reference(xT, w, b, offs):
    idx = unstriped(offs)
    xq = mxq(f64(xT)[:, idx], 0, "e4m3")
    wq = mxq(f64(w), 1, "e4m3")
    y = sum(wq[d].T @ xq[:, d * V:(d + 1) * V] for d in range(D))
    y = relu(y + f64(b))
    return y

@@ -1,0 +1,133 @@
+from contextlib import ExitStack
+
+import concourse.mybir as mybir
+
+F32 = mybir.dt.float32
+BF16 = mybir.dt.bfloat16
+U32 = mybir.dt.uint32
+U16 = mybir.dt.uint16
+U8 = mybir.dt.uint8
+FP8X4 = mybir.dt.float8_e4m3fn_x4
+RELU = mybir.ActivationFunctionType.Relu
+ADD = mybir.AluOpType.add
+MAX = mybir.AluOpType.max
+
+K, T, D, V, N = 512, 4096, 3, 1024, 512
+FLOPS = 2 * K * N * D * V
+
+P = 128
+J = 4
+CHUNKS = ((0, 256), (256, 256), (512, 512), (1024, 512), (1536, 512), (2048, 512), (2560, 512), (3072, 512), (3584, 512))
+VX = (96, 96, 192, 192, 64, 64, 64, 64, 384)
+PIECES = ((0, 0, 256), (1, 0, 256), (2, 0, 256), (0, 256, 256), (1, 256, 256), (2, 256, 256))
+VW = (0, 0, 0, 0, 0, 64)
+HALF = 512
+DMA_ORDER = (('x', 0), ('x', 1), ('x', 2), ('x', 3), ('x', 4), ('x', 5), ('x', 6), ('x', 7), ('x', 8), ('w', 0), ('w', 1), ('w', 2), ('w', 3), ('w', 4), ('w', 5))
+PROG = (('x', 0), ('x', 1), ('x', 2), ('x', 3), ('g', 0, 256, 0), ('x', 4), ('g', 0, 256, 1), ('x', 5), ('g', 0, 256, 2), ('x', 6), ('g', 256, 256, 0), ('x', 7), ('g', 256, 256, 1), ('x', 8), ('g', 256, 256, 2), ('w', 0), ('wq', 0), ('w', 1), ('wq', 1), ('w', 2), ('wq', 2), ('w', 3), ('wq', 3), ('w', 4), ('wq', 4), ('w', 5), ('wq', 5), ('g', 512, 512, 0), ('g', 512, 512, 1), ('g', 512, 512, 2))
+MMS = ((0, 0, 0), (0, 0, 1), (0, 0, 2), (0, 0, 3), (0, 1, 0), (0, 1, 1), (0, 1, 2), (0, 1, 3), (1, 0, 0), (1, 0, 1), (1, 0, 2), (1, 0, 3), (1, 1, 0), (1, 1, 1), (1, 1, 2), (1, 1, 3), (2, 0, 0), (2, 0, 1), (2, 0, 2), (2, 0, 3), (2, 1, 0), (2, 1, 1), (2, 1, 2), (2, 1, 3))
+OUTS = ((0, 0), (1, 0), (2, 0), (3, 0), (0, 1), (1, 1), (2, 1), (3, 1))
+OUTV = [(1, 1), (3, 1)]
+
+
+def interleave(copy, dst, src, a, b):
+    if b > a:
+        copy(
+            out=dst[:, a:b, :].rearrange("p (c i) j -> p c j i", i=4),
+            in_=src[:, :, a:b].rearrange("p j (c i) -> p c j i", i=4),
+        )
+
+
+def tile_picked_deform_lin_relu_def_e_kernel(tc, xT, w, b, offs, out):
+    nc = tc.nc
+    with ExitStack() as ctx:
+        keep = ctx.enter_context(tc.tile_pool(name="keep", bufs=1))
+        psum = ctx.enter_context(tc.psum_pool(name="psum", bufs=1))
+
+        lists = keep.tile([P, D * V // 16], U16, name="lists")
+        bias = keep.tile([P, 4], F32, name="bias")
+        x_words = keep.tile([P, T], U32, name="x_words", align_bytes=64)
+        x_bytes = keep.tile([P, T], U8, name="x_bytes", align_bytes=64)
+
+        xv = xT.rearrange("(p j) t -> p j t", j=J)
+        raw, wraw = {}, {}
+        for n_dma, (kind, i) in enumerate(DMA_ORDER):
+            if kind == "x":
+                c0, n = CHUNKS[i]
+                t = keep.tile([P, J, n], F32, name="xraw%d" % i)
+                nc.sync.dma_start(out=t[:], in_=xv[:, :, c0:c0 + n])
+                raw[i] = t
+            else:
+                d, m0, mc = PIECES[i]
+                t = keep.tile([P, J, mc], F32, name="wraw%d" % i)
+                nc.sync.dma_start(out=t[:], in_=w[d].rearrange("(p j) m -> p j m", j=J)[:, :, m0:m0 + mc])
+                wraw[i] = t
+            if n_dma == 1:
+                nc.sync.dma_start(lists[:], offs)
+        with nc.allow_non_contiguous_dma(reason="512 bias values"):
+            nc.sync.dma_start(out=bias[:], in_=b.rearrange("(m p) o -> p (m o)", p=P))
+
+        gw, gb = {}, {}
+        for d in range(D):
+            for h in range(2):
+                tw = keep.tile([P, HALF], U32, name="gw%d_%d" % (h, d), align_bytes=64)
+                tb = keep.tile([P, HALF], U8, name="gb%d_%d" % (h, d), align_bytes=64)
+                gw[h, d], gb[h, d] = tw, tb
+        wwords, wbytes, wg = {}, {}, {}
+
+        for op in PROG:
+            if op[0] == "x":
+                i = op[1]
+                c0, n = CHUNKS[i]
+                g = keep.tile([P, n, J], BF16, name="xg%d" % i, align_bytes=64)
+                cut = n - VX[i]
+                interleave(nc.scalar.copy, g, raw[i], 0, cut)
+                interleave(nc.vector.tensor_copy, g, raw[i], cut, n)
+                nc.vector.quantize_mx(out=x_words[:, c0:c0 + n].bitcast(FP8X4), scales=x_bytes[:, c0:c0 + n], in_=g[:].rearrange("p c j -> p (c j)"))
+            elif op[0] == "g":
+                v0, n, d = op[1:]
+                h, a = v0 // HALF, v0 % HALF
+                o0 = (d * V + v0) // 16
+                where = lists[:, o0:o0 + n // 16]
+                end = 4 * (v0 + n)
+                nc.vector.tensor_copy(gw[h, d][:, a:a + n], x_words[:, 0:end].indirect(where))
+                nc.vector.tensor_copy(gb[h, d][:, a:a + n], x_bytes[:, 0:end].indirect(where))
+            elif op[0] == "w":
+                i = op[1]
+                d, m0, mc = PIECES[i]
+                g = keep.tile([P, mc, J], BF16, name="wg%d" % i, align_bytes=64)
+                cut = mc - VW[i]
+                interleave(nc.scalar.copy, g, wraw[i], 0, cut)
+                interleave(nc.vector.tensor_copy, g, wraw[i], cut, mc)
+                wg[i] = g
+            else:
+                i = op[1]
+                d, m0, mc = PIECES[i]
+                ww = keep.tile([P, mc], U32, name="ww%d" % i, align_bytes=64)
+                wb = keep.tile([P, mc], U8, name="wb%d" % i, align_bytes=64)
+                nc.vector.quantize_mx(out=ww[:].bitcast(FP8X4), scales=wb[:], in_=wg[i][:].rearrange("p c j -> p (c j)"))
+                for m in range(mc // P):
+                    wwords[d, m0 // P + m] = ww[:, m * P:(m + 1) * P]
+                    wbytes[d, m0 // P + m] = wb[:, m * P:(m + 1) * P]
+
+        banks = {}
+        for m in range(4):
+            for h in range(2):
+                bank = psum.tile([P, HALF], F32, name="bank%d_%d" % (m, h))
+                banks[m, h] = bank
+        for d, h, m in MMS:
+            nc.tensor.matmul_mx(
+                out=banks[m, h][:],
+                lhsT=wwords[d, m].bitcast(FP8X4),
+                lhsT_scale=wbytes[d, m],
+                rhs=gw[h, d][:].bitcast(FP8X4),
+                rhs_scale=gb[h, d][:],
+                start=(d == 0),
+                stop=(d == D - 1),
+            )
+        for m, h in OUTS:
+            y = keep.tile([P, HALF], F32, name="y%d_%d" % (m, h))
+            if (m, h) in OUTV:
+                nc.vector.tensor_scalar(out=y[:], in0=banks[m, h][:], scalar1=bias[:, m:m + 1], scalar2=0.0, op0=ADD, op1=MAX)
+            else:
+                nc.scalar.activation(out=y[:], in_=banks[m, h][:], func=RELU, bias=bias[:, m:m + 1], scale=1.0)
+            nc.sync.dma_start(out=out[m * P:(m + 1) * P, h * HALF:(h + 1) * HALF], in_=y[:])

@@ -18,12 +18,13 @@ FLOPS = 2 * K * N * D * V
 P = 128
 J = 4
 CHUNKS = ((0, 256), (256, 256), (512, 512), (1024, 512), (1536, 512), (2048, 512), (2560, 512), (3072, 512), (3584, 512))
-VX = (96, 96, 192, 192, 64, 64, 64, 64, 384)
+VX = (128, 128, 256, 256, 256, 0, 0, 0, 320)
 PIECES = ((0, 0, 256), (1, 0, 256), (2, 0, 256), (0, 256, 256), (1, 256, 256), (2, 256, 256))
 VW = (0, 0, 0, 0, 0, 64)
 HALF = 512
 DMA_ORDER = (('x', 0), ('x', 1), ('x', 2), ('x', 3), ('x', 4), ('x', 5), ('x', 6), ('x', 7), ('x', 8), ('w', 0), ('w', 1), ('w', 2), ('w', 3), ('w', 4), ('w', 5))
-PROG = (('x', 0), ('x', 1), ('x', 2), ('x', 3), ('g', 0, 256, 0), ('x', 4), ('g', 0, 256, 1), ('x', 5), ('g', 0, 256, 2), ('x', 6), ('g', 256, 256, 0), ('x', 7), ('g', 256, 256, 1), ('x', 8), ('g', 256, 256, 2), ('w', 0), ('wq', 0), ('w', 1), ('wq', 1), ('w', 2), ('wq', 2), ('w', 3), ('wq', 3), ('w', 4), ('wq', 4), ('w', 5), ('wq', 5), ('g', 512, 512, 0), ('g', 512, 512, 1), ('g', 512, 512, 2))
+SHARE = {(1, 0): (0, 1), (1, 1): (2, 3), (1, 2): (4, 5)}
+PROG = (('x', 0), ('x', 1), ('g', 0, 128, 0), ('x', 2), ('g', 0, 128, 1), ('x', 3), ('g', 0, 128, 2), ('x', 4), ('g', 128, 128, 0), ('x', 5), ('g', 128, 128, 1), ('x', 6), ('g', 128, 128, 2), ('x', 7), ('g', 256, 256, 0), ('x', 8), ('g', 256, 256, 1), ('g', 256, 256, 2), ('w', 0), ('w', 1), ('w', 2), ('w', 3), ('w', 4), ('w', 5), ('wq', 0), ('wq', 1), ('g', 512, 512, 0), ('wq', 2), ('wq', 3), ('g', 512, 512, 1), ('wq', 4), ('wq', 5), ('g', 512, 512, 2))
 MMS = ((0, 0, 0), (0, 0, 1), (0, 0, 2), (0, 0, 3), (0, 1, 0), (0, 1, 1), (0, 1, 2), (0, 1, 3), (1, 0, 0), (1, 0, 1), (1, 0, 2), (1, 0, 3), (1, 1, 0), (1, 1, 1), (1, 1, 2), (1, 1, 3), (2, 0, 0), (2, 0, 1), (2, 0, 2), (2, 0, 3), (2, 1, 0), (2, 1, 1), (2, 1, 2), (2, 1, 3))
 OUTS = ((0, 0), (1, 0), (2, 0), (3, 0), (0, 1), (1, 1), (2, 1), (3, 1))
 OUTV = [(1, 1), (3, 1)]
@@ -69,6 +70,8 @@ def tile_picked_deform_lin_relu_def_e_kernel(tc, xT, w, b, offs, out):
         gw, gb = {}, {}
         for d in range(D):
             for h in range(2):
+                if (h, d) in SHARE:
+                    continue
                 tw = keep.tile([P, HALF], U32, name="gw%d_%d" % (h, d), align_bytes=64)
                 tb = keep.tile([P, HALF], U8, name="gb%d_%d" % (h, d), align_bytes=64)
                 gw[h, d], gb[h, d] = tw, tb
@@ -89,12 +92,16 @@ def tile_picked_deform_lin_relu_def_e_kernel(tc, xT, w, b, offs, out):
                 o0 = (d * V + v0) // 16
                 where = lists[:, o0:o0 + n // 16]
                 end = 4 * (v0 + n)
+                if (h, d) not in gw:
+                    tw = keep.tile([P, HALF], U32, name="gw%d_%d" % (h, d), tag="share%d" % SHARE[h, d][0], align_bytes=64)
+                    tb = keep.tile([P, HALF], U8, name="gb%d_%d" % (h, d), tag="share%d" % SHARE[h, d][1], align_bytes=64)
+                    gw[h, d], gb[h, d] = tw, tb
                 nc.vector.tensor_copy(gw[h, d][:, a:a + n], x_words[:, 0:end].indirect(where))
                 nc.vector.tensor_copy(gb[h, d][:, a:a + n], x_bytes[:, 0:end].indirect(where))
             elif op[0] == "w":
                 i = op[1]
                 d, m0, mc = PIECES[i]
-                g = keep.tile([P, mc, J], BF16, name="wg%d" % i, align_bytes=64)
+                g = keep.tile([P, mc, J], BF16, name="wg%d" % i, tag="share%d" % i, align_bytes=64)
                 cut = mc - VW[i]
                 interleave(nc.scalar.copy, g, wraw[i], 0, cut)
                 interleave(nc.vector.tensor_copy, g, wraw[i], cut, mc)

@@ -1,6 +1,7 @@
 from contextlib import ExitStack
 
 import concourse.mybir as mybir
+from concourse.masks import make_identity
 
 F32 = mybir.dt.float32
 BF16 = mybir.dt.bfloat16
@@ -18,16 +19,18 @@ FLOPS = 2 * K * N * D * V
 P = 128
 J = 4
 CHUNKS = ((0, 256), (256, 256), (512, 512), (1024, 512), (1536, 512), (2048, 512), (2560, 512), (3072, 512), (3584, 512))
-VX = (128, 128, 256, 256, 256, 0, 0, 0, 320)
-PIECES = ((0, 0, 256), (1, 0, 256), (2, 0, 256), (0, 256, 256), (1, 256, 256), (2, 256, 256))
-VW = (0, 0, 0, 0, 0, 64)
+VX = (192, 192, 192, 0, 192, 0, 0, 128, 320)
+PIECES = ((0, 0, 256), (0, 256, 256), (1, 0, 256), (1, 256, 256), (2, 0, 256), (2, 256, 128), (2, 384, 128))
+VW = (0, 0, 0, 0, 0, 0, 0)
 HALF = 512
+LOADS = ((0, 256), (256, 256), (512, 512), (1024, 512), (1536, 512), (2048, 512), (2560, 512), (3072, 512), (3584, 512))
+WLOADS = ((0, 0, 256), (0, 256, 256), (1, 0, 256), (1, 256, 256), (2, 0, 256), (2, 256, 256))
 DMA_ORDER = (('x', 0), ('x', 1), ('x', 2), ('x', 3), ('x', 4), ('x', 5), ('x', 6), ('x', 7), ('x', 8), ('w', 0), ('w', 1), ('w', 2), ('w', 3), ('w', 4), ('w', 5))
-SHARE = {(1, 0): (0, 1), (1, 1): (2, 3), (1, 2): (4, 5)}
-PROG = (('x', 0), ('x', 1), ('g', 0, 128, 0), ('x', 2), ('g', 0, 128, 1), ('x', 3), ('g', 0, 128, 2), ('x', 4), ('g', 128, 128, 0), ('x', 5), ('g', 128, 128, 1), ('x', 6), ('g', 128, 128, 2), ('x', 7), ('g', 256, 256, 0), ('x', 8), ('g', 256, 256, 1), ('g', 256, 256, 2), ('w', 0), ('w', 1), ('w', 2), ('w', 3), ('w', 4), ('w', 5), ('wq', 0), ('wq', 1), ('g', 512, 512, 0), ('wq', 2), ('wq', 3), ('g', 512, 512, 1), ('wq', 4), ('wq', 5), ('g', 512, 512, 2))
-MMS = ((0, 0, 0), (0, 0, 1), (0, 0, 2), (0, 0, 3), (0, 1, 0), (0, 1, 1), (0, 1, 2), (0, 1, 3), (1, 0, 0), (1, 0, 1), (1, 0, 2), (1, 0, 3), (1, 1, 0), (1, 1, 1), (1, 1, 2), (1, 1, 3), (2, 0, 0), (2, 0, 1), (2, 0, 2), (2, 0, 3), (2, 1, 0), (2, 1, 1), (2, 1, 2), (2, 1, 3))
-OUTS = ((0, 0), (1, 0), (2, 0), (3, 0), (0, 1), (1, 1), (2, 1), (3, 1))
-OUTV = [(1, 1), (3, 1)]
+SHARE = {(1, 0): (0, None), (1, 1): (1, 5), (1, 2): (3, 6)}
+PROG = (('x', 0), ('x', 1), ('g', 0, 128, 0), ('x', 2), ('g', 0, 128, 1), ('x', 3), ('g', 0, 128, 2), ('x', 4), ('g', 128, 128, 0), ('x', 5), ('g', 128, 128, 1), ('x', 6), ('g', 128, 128, 2), ('x', 7), ('g', 256, 256, 0), ('x', 8), ('g', 256, 256, 1), ('g', 256, 256, 2), ('w', 0), ('w', 1), ('w', 2), ('w', 3), ('w', 4), ('w', 5), ('w', 6), ('wq', 0), ('wq', 1), ('wq', 2), ('wq', 3), ('wq', 4), ('wq', 5), ('wq', 6), ('g', 512, 512, 0), ('g', 512, 512, 1), ('g', 512, 512, 2))
+MMS = ((0, 0, 0), (0, 0, 1), (0, 0, 2), (0, 0, 3), (1, 0, 0), (1, 0, 1), (1, 0, 2), (1, 0, 3), (2, 0, 0), (2, 0, 1), (2, 0, 2), (2, 0, 3), (0, 1, 0), (0, 1, 1), (0, 1, 2), (0, 1, 3), (1, 1, 0), (1, 1, 1), (1, 1, 2), (1, 1, 3), (2, 1, 0), (2, 1, 1), (2, 1, 2), (2, 1, 3))
+OUTS = ((0, 0), (1, 0), (0, 1), (1, 1), (2, 0), (3, 0), (2, 1), (3, 1))
+OUTV = [(1, 1), (3, 0)]
 
 
 def interleave(copy, dst, src, a, b):
@@ -44,6 +47,10 @@ def tile_picked_deform_lin_relu_def_e_kernel(tc, xT, w, b, offs, out):
         keep = ctx.enter_context(tc.tile_pool(name="keep", bufs=1))
         psum = ctx.enter_context(tc.psum_pool(name="psum", bufs=1))
 
+        ident = keep.tile([P, P], F32, name="ident")
+        make_identity(nc, ident[:])
+        b_rows = keep.tile([P, P], F32, name="b_rows")
+        nc.gpsimd.memset(b_rows[:], 0.0)
         lists = keep.tile([P, D * V // 16], U16, name="lists")
         bias = keep.tile([P, 4], F32, name="bias")
         x_words = keep.tile([P, T], U32, name="x_words", align_bytes=64)
@@ -53,19 +60,25 @@ def tile_picked_deform_lin_relu_def_e_kernel(tc, xT, w, b, offs, out):
         raw, wraw = {}, {}
         for n_dma, (kind, i) in enumerate(DMA_ORDER):
             if kind == "x":
-                c0, n = CHUNKS[i]
+                c0, n = LOADS[i]
                 t = keep.tile([P, J, n], F32, name="xraw%d" % i)
                 nc.sync.dma_start(out=t[:], in_=xv[:, :, c0:c0 + n])
-                raw[i] = t
+                for k, (a0, an) in enumerate(CHUNKS):
+                    if c0 <= a0 < c0 + n:
+                        raw[k] = t[:, :, a0 - c0:a0 - c0 + an]
             else:
-                d, m0, mc = PIECES[i]
+                d, m0, mc = WLOADS[i]
                 t = keep.tile([P, J, mc], F32, name="wraw%d" % i)
                 nc.sync.dma_start(out=t[:], in_=w[d].rearrange("(p j) m -> p j m", j=J)[:, :, m0:m0 + mc])
-                wraw[i] = t
+                for k, (pd, p0, pn) in enumerate(PIECES):
+                    if pd == d and m0 <= p0 < m0 + mc:
+                        wraw[k] = t[:, :, p0 - m0:p0 - m0 + pn]
             if n_dma == 1:
                 nc.sync.dma_start(lists[:], offs)
-        with nc.allow_non_contiguous_dma(reason="512 bias values"):
-            nc.sync.dma_start(out=bias[:], in_=b.rearrange("(m p) o -> p (m o)", p=P))
+                nc.sync.dma_start(out=b_rows[0:4, :], in_=b.rearrange("(m p) o -> m (p o)", p=P))
+                b_cols = psum.tile([P, P], F32, name="b_cols", tag="bank3_1")
+                nc.tensor.transpose(b_cols[:], b_rows[:], ident[:])
+                nc.scalar.copy(out=bias[:], in_=b_cols[:, 0:4])
 
         gw, gb = {}, {}
         for d in range(D):
@@ -93,8 +106,8 @@ def tile_picked_deform_lin_relu_def_e_kernel(tc, xT, w, b, offs, out):
                 where = lists[:, o0:o0 + n // 16]
                 end = 4 * (v0 + n)
                 if (h, d) not in gw:
-                    tw = keep.tile([P, HALF], U32, name="gw%d_%d" % (h, d), tag="share%d" % SHARE[h, d][0], align_bytes=64)
-                    tb = keep.tile([P, HALF], U8, name="gb%d_%d" % (h, d), tag="share%d" % SHARE[h, d][1], align_bytes=64)
+                    tw = keep.tile([P, HALF], U32, name="gw%d_%d" % (h, d), tag="share%d" % SHARE[h, d][0] if SHARE[h, d][0] is not None else "gw%d_%d" % (h, d), align_bytes=64)
+                    tb = keep.tile([P, HALF], U8, name="gb%d_%d" % (h, d), tag="share%d" % SHARE[h, d][1] if SHARE[h, d][1] is not None else "gb%d_%d" % (h, d), align_bytes=64)
                     gw[h, d], gb[h, d] = tw, tb
                 nc.vector.tensor_copy(gw[h, d][:, a:a + n], x_words[:, 0:end].indirect(where))
                 nc.vector.tensor_copy(gb[h, d][:, a:a + n], x_bytes[:, 0:end].indirect(where))
@@ -119,7 +132,7 @@ def tile_picked_deform_lin_relu_def_e_kernel(tc, xT, w, b, offs, out):
         banks = {}
         for m in range(4):
             for h in range(2):
-                bank = psum.tile([P, HALF], F32, name="bank%d_%d" % (m, h))
+                bank = psum.tile([P, HALF], F32, name="bank%d_%d" % (m, h), tag="bank%d_%d" % (m, h))
                 banks[m, h] = bank
         for d, h, m in MMS:
             nc.tensor.matmul_mx(

from contextlib import ExitStack

import concourse.mybir as mybir
from concourse.masks import make_identity

F32 = mybir.dt.float32
BF16 = mybir.dt.bfloat16
U32 = mybir.dt.uint32
U16 = mybir.dt.uint16
U8 = mybir.dt.uint8
FP8X4 = mybir.dt.float8_e4m3fn_x4
RELU = mybir.ActivationFunctionType.Relu
ADD = mybir.AluOpType.add
MAX = mybir.AluOpType.max

K, T, D, V, N = 512, 4096, 3, 1024, 512
FLOPS = 2 * K * N * D * V

P = 128
J = 4
CHUNKS = ((0, 256), (256, 256), (512, 512), (1024, 512), (1536, 512), (2048, 512), (2560, 512), (3072, 512), (3584, 512))
VX = (192, 192, 192, 0, 192, 0, 0, 128, 320)
PIECES = ((0, 0, 256), (0, 256, 256), (1, 0, 256), (1, 256, 256), (2, 0, 256), (2, 256, 128), (2, 384, 128))
VW = (0, 0, 0, 0, 0, 0, 0)
HALF = 512
LOADS = ((0, 256), (256, 256), (512, 512), (1024, 512), (1536, 512), (2048, 512), (2560, 512), (3072, 512), (3584, 512))
WLOADS = ((0, 0, 256), (0, 256, 256), (1, 0, 256), (1, 256, 256), (2, 0, 256), (2, 256, 256))
DMA_ORDER = (('x', 0), ('x', 1), ('x', 2), ('x', 3), ('x', 4), ('x', 5), ('x', 6), ('x', 7), ('x', 8), ('w', 0), ('w', 1), ('w', 2), ('w', 3), ('w', 4), ('w', 5))
SHARE = {(1, 0): (0, None), (1, 1): (1, 5), (1, 2): (3, 6)}
PROG = (('x', 0), ('x', 1), ('g', 0, 128, 0), ('x', 2), ('g', 0, 128, 1), ('x', 3), ('g', 0, 128, 2), ('x', 4), ('g', 128, 128, 0), ('x', 5), ('g', 128, 128, 1), ('x', 6), ('g', 128, 128, 2), ('x', 7), ('g', 256, 256, 0), ('x', 8), ('g', 256, 256, 1), ('g', 256, 256, 2), ('w', 0), ('w', 1), ('w', 2), ('w', 3), ('w', 4), ('w', 5), ('w', 6), ('wq', 0), ('wq', 1), ('wq', 2), ('wq', 3), ('wq', 4), ('wq', 5), ('wq', 6), ('g', 512, 512, 0), ('g', 512, 512, 1), ('g', 512, 512, 2))
MMS = ((0, 0, 0), (0, 0, 1), (0, 0, 2), (0, 0, 3), (1, 0, 0), (1, 0, 1), (1, 0, 2), (1, 0, 3), (2, 0, 0), (2, 0, 1), (2, 0, 2), (2, 0, 3), (0, 1, 0), (0, 1, 1), (0, 1, 2), (0, 1, 3), (1, 1, 0), (1, 1, 1), (1, 1, 2), (1, 1, 3), (2, 1, 0), (2, 1, 1), (2, 1, 2), (2, 1, 3))
OUTS = ((0, 0), (1, 0), (0, 1), (1, 1), (2, 0), (3, 0), (2, 1), (3, 1))
OUTV = [(1, 1), (3, 0)]


def interleave(copy, dst, src, a, b):
    if b > a:
        copy(
            out=dst[:, a:b, :].rearrange("p (c i) j -> p c j i", i=4),
            in_=src[:, :, a:b].rearrange("p j (c i) -> p c j i", i=4),
        )


def tile_picked_deform_lin_relu_def_e_kernel(tc, xT, w, b, offs, out):
    nc = tc.nc
    with ExitStack() as ctx:
        keep = ctx.enter_context(tc.tile_pool(name="keep", bufs=1))
        psum = ctx.enter_context(tc.psum_pool(name="psum", bufs=1))

        ident = keep.tile([P, P], F32, name="ident")
        make_identity(nc, ident[:])
        b_rows = keep.tile([P, P], F32, name="b_rows")
        nc.gpsimd.memset(b_rows[:], 0.0)
        lists = keep.tile([P, D * V // 16], U16, name="lists")
        bias = keep.tile([P, 4], F32, name="bias")
        x_words = keep.tile([P, T], U32, name="x_words", align_bytes=64)
        x_bytes = keep.tile([P, T], U8, name="x_bytes", align_bytes=64)

        xv = xT.rearrange("(p j) t -> p j t", j=J)
        raw, wraw = {}, {}
        for n_dma, (kind, i) in enumerate(DMA_ORDER):
            if kind == "x":
                c0, n = LOADS[i]
                t = keep.tile([P, J, n], F32, name="xraw%d" % i)
                nc.sync.dma_start(out=t[:], in_=xv[:, :, c0:c0 + n])
                for k, (a0, an) in enumerate(CHUNKS):
                    if c0 <= a0 < c0 + n:
                        raw[k] = t[:, :, a0 - c0:a0 - c0 + an]
            else:
                d, m0, mc = WLOADS[i]
                t = keep.tile([P, J, mc], F32, name="wraw%d" % i)
                nc.sync.dma_start(out=t[:], in_=w[d].rearrange("(p j) m -> p j m", j=J)[:, :, m0:m0 + mc])
                for k, (pd, p0, pn) in enumerate(PIECES):
                    if pd == d and m0 <= p0 < m0 + mc:
                        wraw[k] = t[:, :, p0 - m0:p0 - m0 + pn]
            if n_dma == 1:
                nc.sync.dma_start(lists[:], offs)
                nc.sync.dma_start(out=b_rows[0:4, :], in_=b.rearrange("(m p) o -> m (p o)", p=P))
                b_cols = psum.tile([P, P], F32, name="b_cols", tag="bank3_1")
                nc.tensor.transpose(b_cols[:], b_rows[:], ident[:])
                nc.scalar.copy(out=bias[:], in_=b_cols[:, 0:4])

        gw, gb = {}, {}
        for d in range(D):
            for h in range(2):
                if (h, d) in SHARE:
                    continue
                tw = keep.tile([P, HALF], U32, name="gw%d_%d" % (h, d), align_bytes=64)
                tb = keep.tile([P, HALF], U8, name="gb%d_%d" % (h, d), align_bytes=64)
                gw[h, d], gb[h, d] = tw, tb
        wwords, wbytes, wg = {}, {}, {}

        for op in PROG:
            if op[0] == "x":
                i = op[1]
                c0, n = CHUNKS[i]
                g = keep.tile([P, n, J], BF16, name="xg%d" % i, align_bytes=64)
                cut = n - VX[i]
                interleave(nc.scalar.copy, g, raw[i], 0, cut)
                interleave(nc.vector.tensor_copy, g, raw[i], cut, n)
                nc.vector.quantize_mx(out=x_words[:, c0:c0 + n].bitcast(FP8X4), scales=x_bytes[:, c0:c0 + n], in_=g[:].rearrange("p c j -> p (c j)"))
            elif op[0] == "g":
                v0, n, d = op[1:]
                h, a = v0 // HALF, v0 % HALF
                o0 = (d * V + v0) // 16
                where = lists[:, o0:o0 + n // 16]
                end = 4 * (v0 + n)
                if (h, d) not in gw:
                    tw = keep.tile([P, HALF], U32, name="gw%d_%d" % (h, d), tag="share%d" % SHARE[h, d][0] if SHARE[h, d][0] is not None else "gw%d_%d" % (h, d), align_bytes=64)
                    tb = keep.tile([P, HALF], U8, name="gb%d_%d" % (h, d), tag="share%d" % SHARE[h, d][1] if SHARE[h, d][1] is not None else "gb%d_%d" % (h, d), align_bytes=64)
                    gw[h, d], gb[h, d] = tw, tb
                nc.vector.tensor_copy(gw[h, d][:, a:a + n], x_words[:, 0:end].indirect(where))
                nc.vector.tensor_copy(gb[h, d][:, a:a + n], x_bytes[:, 0:end].indirect(where))
            elif op[0] == "w":
                i = op[1]
                d, m0, mc = PIECES[i]
                g = keep.tile([P, mc, J], BF16, name="wg%d" % i, tag="share%d" % i, align_bytes=64)
                cut = mc - VW[i]
                interleave(nc.scalar.copy, g, wraw[i], 0, cut)
                interleave(nc.vector.tensor_copy, g, wraw[i], cut, mc)
                wg[i] = g
            else:
                i = op[1]
                d, m0, mc = PIECES[i]
                ww = keep.tile([P, mc], U32, name="ww%d" % i, align_bytes=64)
                wb = keep.tile([P, mc], U8, name="wb%d" % i, align_bytes=64)
                nc.vector.quantize_mx(out=ww[:].bitcast(FP8X4), scales=wb[:], in_=wg[i][:].rearrange("p c j -> p (c j)"))
                for m in range(mc // P):
                    wwords[d, m0 // P + m] = ww[:, m * P:(m + 1) * P]
                    wbytes[d, m0 // P + m] = wb[:, m * P:(m + 1) * P]

        banks = {}
        for m in range(4):
            for h in range(2):
                bank = psum.tile([P, HALF], F32, name="bank%d_%d" % (m, h), tag="bank%d_%d" % (m, h))
                banks[m, h] = bank
        for d, h, m in MMS:
            nc.tensor.matmul_mx(
                out=banks[m, h][:],
                lhsT=wwords[d, m].bitcast(FP8X4),
                lhsT_scale=wbytes[d, m],
                rhs=gw[h, d][:].bitcast(FP8X4),
                rhs_scale=gb[h, d][:],
                start=(d == 0),
                stop=(d == D - 1),
            )
        for m, h in OUTS:
            y = keep.tile([P, HALF], F32, name="y%d_%d" % (m, h))
            if (m, h) in OUTV:
                nc.vector.tensor_scalar(out=y[:], in0=banks[m, h][:], scalar1=bias[:, m:m + 1], scalar2=0.0, op0=ADD, op1=MAX)
            else:
                nc.scalar.activation(out=y[:], in_=banks[m, h][:], func=RELU, bias=bias[:, m:m + 1], scale=1.0)
            nc.sync.dma_start(out=out[m * P:(m + 1) * P, h * HALF:(h + 1) * HALF], in_=y[:])
